import numpy as np
import ml_dtypes


def mxq(x, axis, fmt="e4m3"):
    dtype, down = {"e4m3": (ml_dtypes.float8_e4m3fn, 7), "e5m2": (ml_dtypes.float8_e5m2, 14)}[fmt]
    v = np.moveaxis(np.asarray(x, np.float32).astype(ml_dtypes.bfloat16).astype(np.float64), axis, -1)
    blocks = v.reshape(v.shape[:-1] + (-1, 32))
    amax = np.abs(blocks).max(-1, keepdims=True)
    byte = np.maximum(np.where(amax > 0, np.frexp(amax)[1] - 1 + 127, 0) - down, 1)
    scale = np.exp2(byte - 127.0)
    codes = (blocks / scale).astype(np.float32).astype(dtype).astype(np.float64)
    return np.moveaxis((codes * scale).reshape(v.shape), -1, axis)


WIDE = False


def mx_kscale(k):
    if not WIDE:
        return np.ones(k)
    levels = np.array([30, -30])
    if k % 512:
        return np.exp2(np.random.permutation(np.resize(levels, k // 32))).repeat(32)
    a = np.empty((k // 512, 16))
    for p in range(k // 512):
        a[p, :8] = np.random.permutation(np.resize(levels, 8))
        for g in range(8):
            far = levels[np.abs(levels - a[p, g]) >= 10]
            a[p, g + 8] = far[np.random.randint(len(far))]
    return np.exp2(a.ravel()).repeat(32)


def f64(x):
    return np.asarray(x).astype(np.float64)


def striped(idx):
    return np.tile(np.asarray(idx).reshape(-1, 16).T, (8, 1)).astype(np.uint16)


def unstriped(offs):
    return offs[:16].T.reshape(-1).astype(np.int64)


K, J, N, T, V, Q = 256, 1024, 256, 2048, 2048, 64


def setup_inputs():
    n = np.random.standard_normal
    idx = np.random.permutation(T)[:J]
    idx2 = np.random.permutation(V)[:J]
    fj = mx_kscale(J)
    return {
        "xf": (n((K, T))).astype(np.float32),
        "ra": (np.random.uniform(0.5, 1.5, (1, J)) * fj).astype(np.float32),
        "lo": (np.random.uniform(-0.3, 0.5, (K, 1))).astype(np.float32),
        "gt": (n((N, V)) * np.exp(0.5 * n((1, V)))).astype(np.float32),
        "rb": (np.random.uniform(0.5, 1.5, (1, J)) / fj).astype(np.float32),
        "gk": (np.random.uniform(0.5, 2.0, (K, 1))).astype(np.float32),
        "offs": striped(idx),
        "offs2": striped(idx2),
    }


def reference(xf, ra, lo, gt, rb, gk, offs, offs2):
    idx = unstriped(offs)
    idx2 = unstriped(offs2)
    us = np.maximum(f64(xf)[:, idx] - f64(lo), 0.0) * f64(ra)
    uj = us.T
    gs = f64(gt)[:, idx2] * f64(rb)
    gj = gs.T
    ujq = mxq(uj, 0, "e4m3")
    gjq = mxq(gj, 0, "e5m2")
    w = ujq.T @ gjq
    wq = w.reshape(K, Q, N // Q).sum(axis=2)
    y = 0.02 * wq * f64(gk)
    return y

@@ -1,0 +1,249 @@
+from contextlib import ExitStack
+
+import concourse.mybir as mybir
+
+K, J, N, T, Q = 256, 1024, 256, 2048, 64
+FLOPS = 2 * K * J * N
+
+F32 = mybir.dt.float32
+BF16 = mybir.dt.bfloat16
+U32 = mybir.dt.uint32
+U16 = mybir.dt.uint16
+U8 = mybir.dt.uint8
+E4M3 = mybir.dt.float8_e4m3fn_x4
+E5M2 = mybir.dt.float8_e5m2_x4
+ALU = mybir.AluOpType
+ACT = mybir.ActivationFunctionType
+
+P = 128
+PASS = 512
+HALF = 256
+
+
+def tile_list_moment_over_listed_sums_kernel(tc, xf, ra, lo, gt, rb, gk, offs, offs2, out):
+    nc = tc.nc
+    with ExitStack() as ctx:
+        keep = ctx.enter_context(tc.tile_pool(name="keep", bufs=1))
+        psum = ctx.enter_context(tc.psum_pool(name="psum", bufs=1))
+
+        raw_rows = keep.tile([P, PASS], F32, name="raw_rows")
+        nc.sync.dma_start(raw_rows[0:2, :], ra.rearrange("o (a j) -> (o a) j", a=2))
+        nc.sync.dma_start(raw_rows[2:4, :], rb.rearrange("o (a j) -> (o a) j", a=2))
+
+        x_rows = xf.rearrange("(p c) t -> p c t", c=2)
+        g_rows = gt.rearrange("(p h) v -> p h v", h=2)
+        table = [keep.tile([P, T], F32, name="table%d" % i, align_bytes=64) for i in range(4)]
+        x_list = keep.tile([P, J // 16], U16, name="x_list")
+        g_list = keep.tile([P, J // 16], U16, name="g_list")
+        lo_sb = keep.tile([P, 2], F32, name="lo_sb")
+        gk_sb = keep.tile([P, 2], F32, name="gk_sb")
+        nc.sync.dma_start(table[2][:], g_rows[:, 0, :])
+        nc.sync.dma_start(g_list[:], offs2)
+        nc.sync.dma_start(lo_sb[:], lo.rearrange("(p c) o -> p (c o)", c=2))
+        nc.sync.dma_start(gk_sb[:], gk.rearrange("(p c) o -> p (c o)", c=2))
+        nc.sync.dma_start(x_list[:], offs)
+        nc.sync.dma_start(table[0][:], x_rows[:, 0, :])
+        nc.sync.dma_start(table[1][:], x_rows[:, 1, :])
+        nc.sync.dma_start(table[3][:], g_rows[:, 1, :])
+        lists = [x_list, x_list, g_list, g_list]
+
+
+        staged = keep.tile([P, 4, P], F32, name="staged")
+        zero = keep.tile([P, 1], F32, name="zero")
+        nc.vector.memset(zero[:], 0.0)
+        nc.scalar.activation(staged[:].rearrange("p t c -> p (t c)"), zero[:].to_broadcast([P, PASS]), ACT.Copy)
+        ones = keep.tile([P, 32], F32, name="ones")
+        nc.vector.memset(ones[:], 1.0)
+        ident = keep.tile([P, P], F32, name="ident")
+        nc.vector.memset(ident[:], 0.0)
+        column = keep.tile([P, 32], F32, name="column", align_bytes=64)
+        nc.vector.tensor_tensor_scan(column[:], ones[:], ones[:], 0.0, ALU.mult, ALU.add)
+        row = keep.tile([P, 32], F32, name="row", align_bytes=64)
+        nc.vector.transpose(row[:], column[:])
+        for first in range(0, P, 32):
+            quad = slice(first, first + 32)
+            nc.vector.tensor_tensor(ident[quad, quad], column[quad, :], row[quad, :], ALU.is_equal)
+        nc.vector.tensor_copy(
+            staged[0:4].rearrange("r t (b i) -> r b t i", i=8),
+            raw_rows[0:4, :].rearrange("r (b t i) -> r b t i", t=4, i=8),
+        )
+        turned = psum.tile([P, 4, P], F32, name="bank", tag="u1")
+        for t in range(4):
+            nc.tensor.transpose(turned[:, t, :], staged[:, t, :], ident[:])
+        weights = keep.tile([P, 4, 4], F32, name="weights")
+        nc.vector.tensor_copy(weights[:], turned[:, :, 0:4].rearrange("p t r -> p r t"))
+        neg_lo = keep.tile([P, 2], F32, name="neg_lo")
+        nc.scalar.activation(neg_lo[:], lo_sb[:], ACT.Copy, scale=-1.0)
+        factor = keep.tile([P, 2], F32, name="factor")
+        nc.scalar.activation(factor[:], gk_sb[:], ACT.Copy, scale=0.02)
+        rb_wide = {}
+
+        def spread_rb(a, tag):
+            rb_wide[a] = psum.tile([P, 4, P], F32, name="bank", tag=tag)
+            for t in range(4):
+                nc.tensor.transpose(rb_wide[a][:, t, :], weights[:, 2 + a, t : t + 1].to_broadcast([P, P]), ident[:])
+
+        picked = {(i, a): keep.tile([P, PASS], F32, name="picked%d%d" % (i, a), align_bytes=64)
+                  for i, a in ((0, 1), (1, 1), (2, 0), (2, 1), (3, 0), (3, 1))}
+        above = [[keep.tile([P, 4, P], F32, name="above%d%d" % (i, a)) for a in range(2)] for i in range(2)]
+        pairs = [[keep.tile([P, 2, HALF], BF16, name="pairs%d%d" % (h, a)) for a in range(2)] for h in range(2)]
+        grouped_tags = ["table1", "grouped1", "table0", "grouped3"]
+        grouped = [keep.tile([P, 2, PASS], BF16, name="grouped%d" % i, tag=grouped_tags[i], align_bytes=64) for i in range(4)]
+        code_tags = ["picked31", "codes1", "picked30", "codes3"]
+        codes = [keep.tile([P, 2, P], U32, name="codes%d" % i, tag=code_tags[i], align_bytes=64) for i in range(4)]
+        scales = [keep.tile([P, 2, P], U8, name="scales%d" % i, align_bytes=64) for i in range(4)]
+        acc = [psum.tile([P, P], F32, name="acc%d" % c) for c in range(2)]
+        banks = {}
+
+        def gather(engine, i, a, start, count):
+            first = a * PASS + start
+            window = table[i][:].indirect(lists[i][:, first // 16 : (first + count) // 16])
+            dst = picked[(i, a)][:, start : start + count]
+            if engine == "vector":
+                nc.vector.tensor_copy(dst, window)
+            else:
+                nc.scalar.activation(dst, window, ACT.Copy)
+
+        def excess(engine, c, a, start, count):
+            src = picked[(c, a)][:, start : start + count].rearrange("p (b t i) -> p b t i", t=4, i=8)
+            dst = above[c][a][:, :, start // 4 : (start + count) // 4].rearrange("p t (b i) -> p b t i", i=8)
+            if engine == "vector":
+                nc.vector.tensor_scalar(dst, src, lo_sb[:, c : c + 1], 0.0, ALU.subtract, ALU.max)
+            else:
+                nc.scalar.activation(dst, src, ACT.Relu, bias=neg_lo[:, c : c + 1])
+
+        def turn_x(c, a, tag):
+            bank = psum.tile([P, 4, P], F32, name="bank", tag=tag)
+            for t in range(4):
+                nc.tensor.transpose(bank[:, t, :], above[c][a][:, t, :], ident[:])
+            banks[(c, a)] = bank
+
+        def weigh_x(c, a):
+            nc.vector.tensor_tensor(
+                grouped[c][:, a, :].rearrange("p (k t) -> p k t", t=4),
+                banks[(c, a)][:].rearrange("p t k -> p k t"),
+                weights[:, a : a + 1, :].to_broadcast([P, P, 4]),
+                ALU.mult,
+            )
+
+        def weigh_g(h, a):
+            src = picked[(2 + h, a)][:].rearrange("p (b u e i) -> p u b i e", u=2, e=2, i=8)
+            wide = rb_wide[a][:].rearrange("p (u e) (b i) -> p u b i e", e=2, i=8)
+            for u in range(2):
+                dst = pairs[h][a][:, u, :].rearrange("p (b i e) -> p b i e", i=8, e=2)
+                nc.vector.tensor_tensor(dst, src[:, u], wide[:, u], ALU.mult)
+
+        def turn_g(h, a, tag):
+            bank = psum.tile([P, 4, P], F32, name="bank", tag=tag)
+            for u in range(2):
+                nc.tensor.transpose(bank[:, u, :], pairs[h][a][:, u, :].bitcast(F32), ident[:])
+            banks[(2 + h, a)] = bank
+
+        def collect_g(engine, h, a):
+            dst = grouped[2 + h][:, a, :].bitcast(F32).rearrange("p (n u) -> p n u", u=2)
+            src = banks[(2 + h, a)][:, 0:2, :].rearrange("p u n -> p n u")
+            if engine == "vector":
+                nc.vector.tensor_copy(dst, src)
+            else:
+                nc.scalar.copy(dst, src)
+
+        def quantize(i, first, last):
+            fmt = E4M3 if i < 2 else E5M2
+            nc.vector.quantize_mx(
+                out=codes[i][:, first:last, :].rearrange("p a c -> p (a c)").bitcast(fmt),
+                scales=scales[i][:, first:last, :].rearrange("p a c -> p (a c)"),
+                in_=grouped[i][:, first:last, :].rearrange("p a c -> p (a c)"),
+            )
+
+        def multiply(h, a, cs=(0, 1)):
+            for c in cs:
+                nc.tensor.matmul_mx(
+                    out=acc[c][:],
+                    lhsT=codes[c][:, a, :].bitcast(E4M3),
+                    lhsT_scale=scales[c][:, a, :],
+                    rhs=codes[2 + h][:, a, :].bitcast(E5M2),
+                    rhs_scale=scales[2 + h][:, a, :],
+                    start=(h == 0 and a == 0),
+                    stop=(h == 1 and a == 1),
+                )
+
+        def gather_turnable(c, a):
+            window = table[c][:].bitcast(U32).indirect(lists[c][:, a * PASS // 16 : (a + 1) * PASS // 16])
+            nc.vector.tensor_copy(above[c][a][:].bitcast(U32).rearrange("p t (b i) -> p b t i", i=8), window)
+
+        def open_x(c, a, tag):
+            bank = psum.tile([P, 4, P], F32, name="bank", tag=tag)
+            for t in range(4):
+                nc.tensor.matmul(bank[:, t, :], neg_lo[:, c : c + 1].to_broadcast([P, P]), ident[:],
+                                 is_transpose=True, start=(t == 0), stop=False)
+            banks[(c, a)] = bank
+
+        def add_x(c, a):
+            for t in range(4):
+                nc.tensor.matmul(banks[(c, a)][:, t, :], above[c][a][:, t, :], ident[:],
+                                 is_transpose=True, start=False, stop=(t == 3))
+
+        def clip_weigh_x(c, a):
+            nc.vector.scalar_tensor_tensor(
+                grouped[c][:, a, :].rearrange("p (k t) -> p k t", t=4),
+                banks[(c, a)][:].rearrange("p t k -> p k t"),
+                0.0,
+                weights[:, a : a + 1, :].to_broadcast([P, P, 4]),
+                ALU.max,
+                ALU.mult,
+            )
+
+        spread_rb(0, "u3")
+        spread_rb(1, "u4")
+        gather("vector", 2, 0, 0, PASS)
+        gather("scalar", 2, 1, 0, PASS)
+        weigh_g(0, 0)
+        turn_g(0, 0, "u1")
+        weigh_g(0, 1)
+        open_x(0, 0, "u2")
+        turn_g(0, 1, "u6")
+        open_x(1, 0, "u5")
+        gather("scalar", 0, 1, 0, PASS)
+        gather_turnable(0, 0)
+        excess("scalar", 0, 1, 0, PASS)
+        collect_g("vector", 0, 0)
+        collect_g("vector", 0, 1)
+        add_x(0, 0)
+        turn_x(0, 1, "u1")
+        gather("scalar", 1, 1, 0, PASS)
+        gather_turnable(1, 0)
+        excess("scalar", 1, 1, 0, PASS)
+        clip_weigh_x(0, 0)
+        weigh_x(0, 1)
+        add_x(1, 0)
+        turn_x(1, 1, "u6")
+        clip_weigh_x(1, 0)
+        gather("scalar", 3, 0, 0, PASS)
+        gather("scalar", 3, 1, 0, HALF)
+        gather("vector", 3, 1, HALF, HALF)
+        weigh_x(1, 1)
+        weigh_g(1, 0)
+        turn_g(1, 0, "u2")
+        weigh_g(1, 1)
+        turn_g(1, 1, "u1")
+        quantize(2, 0, 2)
+        quantize(1, 0, 2)
+        quantize(0, 0, 2)
+        collect_g("scalar", 1, 0)
+        quantize(3, 0, 1)
+        collect_g("scalar", 1, 1)
+        multiply(0, 0, (1,))
+        multiply(0, 1, (1,))
+        multiply(0, 0, (0,))
+        multiply(0, 1, (0,))
+        multiply(1, 0)
+        quantize(3, 1, 2)
+        multiply(1, 1)
+
+        scaled = keep.tile([P, 2, P], F32, name="scaled")
+        nc.scalar.activation(scaled[:, 0, :], acc[0][:], ACT.Copy, scale=factor[:, 0:1])
+        nc.vector.tensor_scalar(scaled[:, 1, :], acc[1][:], factor[:, 1:2], None, ALU.mult)
+        result = keep.tile([P, 2 * Q], F32, name="result")
+        halves = scaled[:].rearrange("p c (q e) -> p (c q) e", e=2)
+        nc.vector.tensor_tensor(result[:], halves[:, :, 0], halves[:, :, 1], ALU.add)
+        nc.sync.dma_start(out.rearrange("(p c) q -> p (c q)", c=2), result[:])

@@ -29,37 +29,36 @@ def tile_list_moment_over_listed_sums_kernel(tc, xf, ra, lo, gt, rb, gk, offs, o
         raw_rows = keep.tile([P, PASS], F32, name="raw_rows")
         nc.sync.dma_start(raw_rows[0:2, :], ra.rearrange("o (a j) -> (o a) j", a=2))
         nc.sync.dma_start(raw_rows[2:4, :], rb.rearrange("o (a j) -> (o a) j", a=2))
+        nc.sync.dma_start(raw_rows[32:33, 0:K], lo.rearrange("k o -> o k"))
 
         x_rows = xf.rearrange("(p c) t -> p c t", c=2)
         g_rows = gt.rearrange("(p h) v -> p h v", h=2)
         table = [keep.tile([P, T], F32, name="table%d" % i, align_bytes=64) for i in range(4)]
         x_list = keep.tile([P, J // 16], U16, name="x_list")
         g_list = keep.tile([P, J // 16], U16, name="g_list")
-        lo_sb = keep.tile([P, 2], F32, name="lo_sb")
         gk_sb = keep.tile([P, 2], F32, name="gk_sb")
         nc.sync.dma_start(table[2][:], g_rows[:, 0, :])
         nc.sync.dma_start(g_list[:], offs2)
-        nc.sync.dma_start(lo_sb[:], lo.rearrange("(p c) o -> p (c o)", c=2))
-        nc.sync.dma_start(gk_sb[:], gk.rearrange("(p c) o -> p (c o)", c=2))
         nc.sync.dma_start(x_list[:], offs)
         nc.sync.dma_start(table[0][:], x_rows[:, 0, :])
         nc.sync.dma_start(table[1][:], x_rows[:, 1, :])
         nc.sync.dma_start(table[3][:], g_rows[:, 1, :])
+        nc.sync.dma_start(gk_sb[:], gk.rearrange("(p c) o -> p (c o)", c=2))
         lists = [x_list, x_list, g_list, g_list]
 
 
         staged = keep.tile([P, 4, P], F32, name="staged")
         zero = keep.tile([P, 1], F32, name="zero")
         nc.vector.memset(zero[:], 0.0)
-        nc.scalar.activation(staged[:].rearrange("p t c -> p (t c)"), zero[:].to_broadcast([P, PASS]), ACT.Copy)
+        ident = keep.tile([P, P], F32, name="ident")
+        nc.scalar.activation(ident[:], zero[:].to_broadcast([P, P]), ACT.Copy)
         ones = keep.tile([P, 32], F32, name="ones")
         nc.vector.memset(ones[:], 1.0)
-        ident = keep.tile([P, P], F32, name="ident")
-        nc.vector.memset(ident[:], 0.0)
         column = keep.tile([P, 32], F32, name="column", align_bytes=64)
         nc.vector.tensor_tensor_scan(column[:], ones[:], ones[:], 0.0, ALU.mult, ALU.add)
         row = keep.tile([P, 32], F32, name="row", align_bytes=64)
         nc.vector.transpose(row[:], column[:])
+        nc.vector.memset(staged[:], 0.0)
         for first in range(0, P, 32):
             quad = slice(first, first + 32)
             nc.vector.tensor_tensor(ident[quad, quad], column[quad, :], row[quad, :], ALU.is_equal)
@@ -67,15 +66,19 @@ def tile_list_moment_over_listed_sums_kernel(tc, xf, ra, lo, gt, rb, gk, offs, o
             staged[0:4].rearrange("r t (b i) -> r b t i", i=8),
             raw_rows[0:4, :].rearrange("r (b t i) -> r b t i", t=4, i=8),
         )
+        nc.vector.tensor_copy(staged[32:33, 0:2, :], raw_rows[32:33, 0:K].rearrange("r (p c) -> r c p", c=2))
         turned = psum.tile([P, 4, P], F32, name="bank", tag="u1")
         for t in range(4):
             nc.tensor.transpose(turned[:, t, :], staged[:, t, :], ident[:])
         weights = keep.tile([P, 4, 4], F32, name="weights")
         nc.vector.tensor_copy(weights[:], turned[:, :, 0:4].rearrange("p t r -> p r t"))
         neg_lo = keep.tile([P, 2], F32, name="neg_lo")
-        nc.scalar.activation(neg_lo[:], lo_sb[:], ACT.Copy, scale=-1.0)
-        factor = keep.tile([P, 2], F32, name="factor")
-        nc.scalar.activation(factor[:], gk_sb[:], ACT.Copy, scale=0.02)
+        nc.scalar.activation(neg_lo[:], turned[:, 0:2, 32], ACT.Copy, scale=-1.0)
+        row_factor = keep.tile([P, 2], F32, name="row_factor")
+
+        def factor():
+            nc.scalar.activation(row_factor[:], gk_sb[:], ACT.Copy, scale=0.02)
+
         rb_wide = {}
 
         def spread_rb(a, tag):
@@ -86,12 +89,13 @@ def tile_list_moment_over_listed_sums_kernel(tc, xf, ra, lo, gt, rb, gk, offs, o
         picked = {(i, a): keep.tile([P, PASS], F32, name="picked%d%d" % (i, a), align_bytes=64)
                   for i, a in ((0, 1), (1, 1), (2, 0), (2, 1), (3, 0), (3, 1))}
         above = [[keep.tile([P, 4, P], F32, name="above%d%d" % (i, a)) for a in range(2)] for i in range(2)]
-        pairs = [[keep.tile([P, 2, HALF], BF16, name="pairs%d%d" % (h, a)) for a in range(2)] for h in range(2)]
+        pairs = {(h, a, u): keep.tile([P, HALF], BF16, name="pairs%d%d%d" % (h, a, u))
+                 for h in range(2) for a in range(2) for u in range(2)}
         grouped_tags = ["table1", "grouped1", "table0", "grouped3"]
-        grouped = [keep.tile([P, 2, PASS], BF16, name="grouped%d" % i, tag=grouped_tags[i], align_bytes=64) for i in range(4)]
+        grouped = [keep.tile([P, J], BF16, name="grouped%d" % i, tag=grouped_tags[i], align_bytes=64) for i in range(4)]
         code_tags = ["picked31", "codes1", "picked30", "codes3"]
-        codes = [keep.tile([P, 2, P], U32, name="codes%d" % i, tag=code_tags[i], align_bytes=64) for i in range(4)]
-        scales = [keep.tile([P, 2, P], U8, name="scales%d" % i, align_bytes=64) for i in range(4)]
+        codes = [keep.tile([P, 2 * P], U32, name="codes%d" % i, tag=code_tags[i], align_bytes=64) for i in range(4)]
+        scales = [keep.tile([P, 2 * P], U8, name="scales%d" % i, align_bytes=64) for i in range(4)]
         acc = [psum.tile([P, P], F32, name="acc%d" % c) for c in range(2)]
         banks = {}
 
@@ -108,7 +112,7 @@ def tile_list_moment_over_listed_sums_kernel(tc, xf, ra, lo, gt, rb, gk, offs, o
             src = picked[(c, a)][:, start : start + count].rearrange("p (b t i) -> p b t i", t=4, i=8)
             dst = above[c][a][:, :, start // 4 : (start + count) // 4].rearrange("p t (b i) -> p b t i", i=8)
             if engine == "vector":
-                nc.vector.tensor_scalar(dst, src, lo_sb[:, c : c + 1], 0.0, ALU.subtract, ALU.max)
+                nc.vector.tensor_scalar(dst, src, neg_lo[:, c : c + 1], 0.0, ALU.add, ALU.max)
             else:
                 nc.scalar.activation(dst, src, ACT.Relu, bias=neg_lo[:, c : c + 1])
 
@@ -120,7 +124,7 @@ def tile_list_moment_over_listed_sums_kernel(tc, xf, ra, lo, gt, rb, gk, offs, o
 
         def weigh_x(c, a):
             nc.vector.tensor_tensor(
-                grouped[c][:, a, :].rearrange("p (k t) -> p k t", t=4),
+                grouped[c][:, a * PASS : (a + 1) * PASS].rearrange("p (k t) -> p k t", t=4),
                 banks[(c, a)][:].rearrange("p t k -> p k t"),
                 weights[:, a : a + 1, :].to_broadcast([P, P, 4]),
                 ALU.mult,
@@ -130,17 +134,25 @@ def tile_list_moment_over_listed_sums_kernel(tc, xf, ra, lo, gt, rb, gk, offs, o
             src = picked[(2 + h, a)][:].rearrange("p (b u e i) -> p u b i e", u=2, e=2, i=8)
             wide = rb_wide[a][:].rearrange("p (u e) (b i) -> p u b i e", e=2, i=8)
             for u in range(2):
-                dst = pairs[h][a][:, u, :].rearrange("p (b i e) -> p b i e", i=8, e=2)
+                dst = pairs[(h, a, u)][:].rearrange("p (b i e) -> p b i e", i=8, e=2)
                 nc.vector.tensor_tensor(dst, src[:, u], wide[:, u], ALU.mult)
+
+        def weigh_g_half(h, a, half):
+            blocks = slice(8 * half, 8 * half + 8)
+            src = picked[(2 + h, a)][:].rearrange("p (b u e i) -> p u b i e", u=2, e=2, i=8)
+            wide = rb_wide[a][:].rearrange("p (u e) (b i) -> p u b i e", e=2, i=8)
+            for u in range(2):
+                dst = pairs[(h, a, u)][:].rearrange("p (b i e) -> p b i e", i=8, e=2)
+                nc.vector.tensor_tensor(dst[:, blocks], src[:, u, blocks], wide[:, u, blocks], ALU.mult)
 
         def turn_g(h, a, tag):
             bank = psum.tile([P, 4, P], F32, name="bank", tag=tag)
             for u in range(2):
-                nc.tensor.transpose(bank[:, u, :], pairs[h][a][:, u, :].bitcast(F32), ident[:])
+                nc.tensor.transpose(bank[:, u, :], pairs[(h, a, u)][:].bitcast(F32), ident[:])
             banks[(2 + h, a)] = bank
 
         def collect_g(engine, h, a):
-            dst = grouped[2 + h][:, a, :].bitcast(F32).rearrange("p (n u) -> p n u", u=2)
+            dst = grouped[2 + h][:, a * PASS : (a + 1) * PASS].bitcast(F32).rearrange("p (n u) -> p n u", u=2)
             src = banks[(2 + h, a)][:, 0:2, :].rearrange("p u n -> p n u")
             if engine == "vector":
                 nc.vector.tensor_copy(dst, src)
@@ -150,19 +162,19 @@ def tile_list_moment_over_listed_sums_kernel(tc, xf, ra, lo, gt, rb, gk, offs, o
         def quantize(i, first, last):
             fmt = E4M3 if i < 2 else E5M2
             nc.vector.quantize_mx(
-                out=codes[i][:, first:last, :].rearrange("p a c -> p (a c)").bitcast(fmt),
-                scales=scales[i][:, first:last, :].rearrange("p a c -> p (a c)"),
-                in_=grouped[i][:, first:last, :].rearrange("p a c -> p (a c)"),
+                out=codes[i][:, first * P : last * P].bitcast(fmt),
+                scales=scales[i][:, first * P : last * P],
+                in_=grouped[i][:, first * PASS : last * PASS],
             )
 
         def multiply(h, a, cs=(0, 1)):
             for c in cs:
                 nc.tensor.matmul_mx(
                     out=acc[c][:],
-                    lhsT=codes[c][:, a, :].bitcast(E4M3),
-                    lhsT_scale=scales[c][:, a, :],
-                    rhs=codes[2 + h][:, a, :].bitcast(E5M2),
-                    rhs_scale=scales[2 + h][:, a, :],
+                    lhsT=codes[c][:, a * P : (a + 1) * P].bitcast(E4M3),
+                    lhsT_scale=scales[c][:, a * P : (a + 1) * P],
+                    rhs=codes[2 + h][:, a * P : (a + 1) * P].bitcast(E5M2),
+                    rhs_scale=scales[2 + h][:, a * P : (a + 1) * P],
                     start=(h == 0 and a == 0),
                     stop=(h == 1 and a == 1),
                 )
@@ -185,7 +197,7 @@ def tile_list_moment_over_listed_sums_kernel(tc, xf, ra, lo, gt, rb, gk, offs, o
 
         def clip_weigh_x(c, a):
             nc.vector.scalar_tensor_tensor(
-                grouped[c][:, a, :].rearrange("p (k t) -> p k t", t=4),
+                grouped[c][:, a * PASS : (a + 1) * PASS].rearrange("p (k t) -> p k t", t=4),
                 banks[(c, a)][:].rearrange("p t k -> p k t"),
                 0.0,
                 weights[:, a : a + 1, :].to_broadcast([P, P, 4]),
@@ -205,8 +217,8 @@ def tile_list_moment_over_listed_sums_kernel(tc, xf, ra, lo, gt, rb, gk, offs, o
         open_x(1, 0, "u5")
         gather("scalar", 0, 1, 0, PASS)
         gather_turnable(0, 0)
-        excess("scalar", 0, 1, 0, PASS)
-        collect_g("vector", 0, 0)
+        excess("vector", 0, 1, 0, PASS)
+        collect_g("scalar", 0, 0)
         collect_g("vector", 0, 1)
         add_x(0, 0)
         turn_x(0, 1, "u1")
@@ -220,11 +232,13 @@ def tile_list_moment_over_listed_sums_kernel(tc, xf, ra, lo, gt, rb, gk, offs, o
         clip_weigh_x(1, 0)
         gather("scalar", 3, 0, 0, PASS)
         gather("scalar", 3, 1, 0, HALF)
-        gather("vector", 3, 1, HALF, HALF)
+        gather("scalar", 3, 1, HALF, HALF)
+
         weigh_x(1, 1)
         weigh_g(1, 0)
         turn_g(1, 0, "u2")
-        weigh_g(1, 1)
+        weigh_g_half(1, 1, 0)
+        weigh_g_half(1, 1, 1)
         turn_g(1, 1, "u1")
         quantize(2, 0, 2)
         quantize(1, 0, 2)
@@ -237,12 +251,13 @@ def tile_list_moment_over_listed_sums_kernel(tc, xf, ra, lo, gt, rb, gk, offs, o
         multiply(0, 0, (0,))
         multiply(0, 1, (0,))
         multiply(1, 0)
+        factor()
         quantize(3, 1, 2)
         multiply(1, 1)
 
         scaled = keep.tile([P, 2, P], F32, name="scaled")
-        nc.scalar.activation(scaled[:, 0, :], acc[0][:], ACT.Copy, scale=factor[:, 0:1])
-        nc.vector.tensor_scalar(scaled[:, 1, :], acc[1][:], factor[:, 1:2], None, ALU.mult)
+        nc.scalar.activation(scaled[:, 0, :], acc[0][:], ACT.Copy, scale=row_factor[:, 0:1])
+        nc.vector.tensor_scalar(scaled[:, 1, :], acc[1][:], row_factor[:, 1:2], None, ALU.mult)
         result = keep.tile([P, 2 * Q], F32, name="result")
         halves = scaled[:].rearrange("p c (q e) -> p (c q) e", e=2)
         nc.vector.tensor_tensor(result[:], halves[:, :, 0], halves[:, :, 1], ALU.add)

@@ -63,8 +63,8 @@ def tile_list_moment_over_listed_sums_kernel(tc, xf, ra, lo, gt, rb, gk, offs, o
             quad = slice(first, first + 32)
             nc.vector.tensor_tensor(ident[quad, quad], column[quad, :], row[quad, :], ALU.is_equal)
         nc.vector.tensor_copy(
-            staged[0:4].rearrange("r t (b i) -> r b t i", i=8),
-            raw_rows[0:4, :].rearrange("r (b t i) -> r b t i", t=4, i=8),
+            staged[0:4].rearrange("r t q -> r q t"),
+            raw_rows[0:4, :].rearrange("r (q t) -> r q t", t=4),
         )
         nc.vector.tensor_copy(staged[32:33, 0:2, :], raw_rows[32:33, 0:K].rearrange("r (p c) -> r c p", c=2))
         turned = psum.tile([P, 4, P], F32, name="bank", tag="u1")
@@ -87,16 +87,17 @@ def tile_list_moment_over_listed_sums_kernel(tc, xf, ra, lo, gt, rb, gk, offs, o
                 nc.tensor.transpose(rb_wide[a][:, t, :], weights[:, 2 + a, t : t + 1].to_broadcast([P, P]), ident[:])
 
         picked = {(i, a): keep.tile([P, PASS], F32, name="picked%d%d" % (i, a), align_bytes=64)
-                  for i, a in ((0, 1), (1, 1), (2, 0), (2, 1), (3, 0), (3, 1))}
-        above = [[keep.tile([P, 4, P], F32, name="above%d%d" % (i, a)) for a in range(2)] for i in range(2)]
-        pairs = {(h, a, u): keep.tile([P, HALF], BF16, name="pairs%d%d%d" % (h, a, u))
-                 for h in range(2) for a in range(2) for u in range(2)}
-        grouped_tags = ["table1", "grouped1", "table0", "grouped3"]
-        grouped = [keep.tile([P, J], BF16, name="grouped%d" % i, tag=grouped_tags[i], align_bytes=64) for i in range(4)]
-        code_tags = ["picked31", "codes1", "picked30", "codes3"]
+                  for i in range(4) for a in range(2)}
+        pairs = {(h, a): keep.tile([P, PASS], BF16, name="pairs%d%d" % (h, a)) for h in range(2) for a in range(2)}
+        whole = {i: keep.tile([P, J], BF16, name="grouped%d" % i, tag=tag, align_bytes=64)
+                 for i, tag in ((0, "grouped0"), (2, "table0"), (3, "grouped3"))}
+        grouped = {(i, a): whole[i][:, a * PASS : (a + 1) * PASS] for i in whole for a in range(2)}
+        for a, tag in ((0, "grouped1"), (1, "table3")):
+            grouped[(1, a)] = keep.tile([P, PASS], BF16, name="grouped1%d" % a, tag=tag, align_bytes=64)[:]
+        code_tags = ["codes0", "picked31", "codes2", "codes3"]
         codes = [keep.tile([P, 2 * P], U32, name="codes%d" % i, tag=code_tags[i], align_bytes=64) for i in range(4)]
         scales = [keep.tile([P, 2 * P], U8, name="scales%d" % i, align_bytes=64) for i in range(4)]
-        acc = [psum.tile([P, P], F32, name="acc%d" % c) for c in range(2)]
+        acc = {}
         banks = {}
 
         def gather(engine, i, a, start, count):
@@ -108,51 +109,23 @@ def tile_list_moment_over_listed_sums_kernel(tc, xf, ra, lo, gt, rb, gk, offs, o
             else:
                 nc.scalar.activation(dst, window, ACT.Copy)
 
-        def excess(engine, c, a, start, count):
-            src = picked[(c, a)][:, start : start + count].rearrange("p (b t i) -> p b t i", t=4, i=8)
-            dst = above[c][a][:, :, start // 4 : (start + count) // 4].rearrange("p t (b i) -> p b t i", i=8)
-            if engine == "vector":
-                nc.vector.tensor_scalar(dst, src, neg_lo[:, c : c + 1], 0.0, ALU.add, ALU.max)
-            else:
-                nc.scalar.activation(dst, src, ACT.Relu, bias=neg_lo[:, c : c + 1])
-
-        def turn_x(c, a, tag):
-            bank = psum.tile([P, 4, P], F32, name="bank", tag=tag)
-            for t in range(4):
-                nc.tensor.transpose(bank[:, t, :], above[c][a][:, t, :], ident[:])
-            banks[(c, a)] = bank
-
-        def weigh_x(c, a):
+        def weigh_g1(h, a):
             nc.vector.tensor_tensor(
-                grouped[c][:, a * PASS : (a + 1) * PASS].rearrange("p (k t) -> p k t", t=4),
-                banks[(c, a)][:].rearrange("p t k -> p k t"),
-                weights[:, a : a + 1, :].to_broadcast([P, P, 4]),
+                pairs[(h, a)][:].rearrange("p (q t) -> p q t", t=4),
+                picked[(2 + h, a)][:].rearrange("p (q t) -> p q t", t=4),
+                rb_wide[a][:].rearrange("p t q -> p q t"),
                 ALU.mult,
             )
 
-        def weigh_g(h, a):
-            src = picked[(2 + h, a)][:].rearrange("p (b u e i) -> p u b i e", u=2, e=2, i=8)
-            wide = rb_wide[a][:].rearrange("p (u e) (b i) -> p u b i e", e=2, i=8)
-            for u in range(2):
-                dst = pairs[(h, a, u)][:].rearrange("p (b i e) -> p b i e", i=8, e=2)
-                nc.vector.tensor_tensor(dst, src[:, u], wide[:, u], ALU.mult)
-
-        def weigh_g_half(h, a, half):
-            blocks = slice(8 * half, 8 * half + 8)
-            src = picked[(2 + h, a)][:].rearrange("p (b u e i) -> p u b i e", u=2, e=2, i=8)
-            wide = rb_wide[a][:].rearrange("p (u e) (b i) -> p u b i e", e=2, i=8)
-            for u in range(2):
-                dst = pairs[(h, a, u)][:].rearrange("p (b i e) -> p b i e", i=8, e=2)
-                nc.vector.tensor_tensor(dst[:, blocks], src[:, u, blocks], wide[:, u, blocks], ALU.mult)
-
         def turn_g(h, a, tag):
             bank = psum.tile([P, 4, P], F32, name="bank", tag=tag)
+            words = pairs[(h, a)][:].bitcast(F32)
             for u in range(2):
-                nc.tensor.transpose(bank[:, u, :], pairs[(h, a, u)][:].bitcast(F32), ident[:])
+                nc.tensor.transpose(bank[:, u, :], words[:, u:HALF:2], ident[:])
             banks[(2 + h, a)] = bank
 
         def collect_g(engine, h, a):
-            dst = grouped[2 + h][:, a * PASS : (a + 1) * PASS].bitcast(F32).rearrange("p (n u) -> p n u", u=2)
+            dst = grouped[(2 + h, a)].bitcast(F32).rearrange("p (n u) -> p n u", u=2)
             src = banks[(2 + h, a)][:, 0:2, :].rearrange("p u n -> p n u")
             if engine == "vector":
                 nc.vector.tensor_copy(dst, src)
@@ -164,11 +137,13 @@ def tile_list_moment_over_listed_sums_kernel(tc, xf, ra, lo, gt, rb, gk, offs, o
             nc.vector.quantize_mx(
                 out=codes[i][:, first * P : last * P].bitcast(fmt),
                 scales=scales[i][:, first * P : last * P],
-                in_=grouped[i][:, first * PASS : last * PASS],
+                in_=whole[i][:] if last - first == 2 else grouped[(i, first)],
             )
 
         def multiply(h, a, cs=(0, 1)):
             for c in cs:
+                if c not in acc:
+                    acc[c] = psum.tile([P, P], F32, name="acc%d" % c, tag="acc%d" % c)
                 nc.tensor.matmul_mx(
                     out=acc[c][:],
                     lhsT=codes[c][:, a * P : (a + 1) * P].bitcast(E4M3),
@@ -179,10 +154,6 @@ def tile_list_moment_over_listed_sums_kernel(tc, xf, ra, lo, gt, rb, gk, offs, o
                     stop=(h == 1 and a == 1),
                 )
 
-        def gather_turnable(c, a):
-            window = table[c][:].bitcast(U32).indirect(lists[c][:, a * PASS // 16 : (a + 1) * PASS // 16])
-            nc.vector.tensor_copy(above[c][a][:].bitcast(U32).rearrange("p t (b i) -> p b t i", i=8), window)
-
         def open_x(c, a, tag):
             bank = psum.tile([P, 4, P], F32, name="bank", tag=tag)
             for t in range(4):
@@ -190,14 +161,14 @@ def tile_list_moment_over_listed_sums_kernel(tc, xf, ra, lo, gt, rb, gk, offs, o
                                  is_transpose=True, start=(t == 0), stop=False)
             banks[(c, a)] = bank
 
-        def add_x(c, a):
+        def add_s(c, a):
             for t in range(4):
-                nc.tensor.matmul(banks[(c, a)][:, t, :], above[c][a][:, t, :], ident[:],
+                nc.tensor.matmul(banks[(c, a)][:, t, :], picked[(c, a)][:, t:PASS:4], ident[:],
                                  is_transpose=True, start=False, stop=(t == 3))
 
         def clip_weigh_x(c, a):
             nc.vector.scalar_tensor_tensor(
-                grouped[c][:, a * PASS : (a + 1) * PASS].rearrange("p (k t) -> p k t", t=4),
+                grouped[(c, a)].rearrange("p (k t) -> p k t", t=4),
                 banks[(c, a)][:].rearrange("p t k -> p k t"),
                 0.0,
                 weights[:, a : a + 1, :].to_broadcast([P, P, 4]),
@@ -209,48 +180,48 @@ def tile_list_moment_over_listed_sums_kernel(tc, xf, ra, lo, gt, rb, gk, offs, o
         spread_rb(1, "u4")
         gather("vector", 2, 0, 0, PASS)
         gather("scalar", 2, 1, 0, PASS)
-        weigh_g(0, 0)
+        weigh_g1(0, 0)
         turn_g(0, 0, "u1")
-        weigh_g(0, 1)
-        open_x(0, 0, "u2")
+        weigh_g1(0, 1)
         turn_g(0, 1, "u6")
+        open_x(0, 0, "u2")
+        open_x(0, 1, "acc0")
         open_x(1, 0, "u5")
+        open_x(1, 1, "acc1")
+        gather("vector", 0, 0, 0, PASS)
         gather("scalar", 0, 1, 0, PASS)
-        gather_turnable(0, 0)
-        excess("vector", 0, 1, 0, PASS)
-        collect_g("scalar", 0, 0)
+        add_s(0, 0)
+        add_s(0, 1)
+        collect_g("vector", 0, 0)
         collect_g("vector", 0, 1)
-        add_x(0, 0)
-        turn_x(0, 1, "u1")
+        quantize(2, 0, 2)
+        gather("scalar", 1, 0, 0, PASS)
         gather("scalar", 1, 1, 0, PASS)
-        gather_turnable(1, 0)
-        excess("scalar", 1, 1, 0, PASS)
         clip_weigh_x(0, 0)
-        weigh_x(0, 1)
-        add_x(1, 0)
-        turn_x(1, 1, "u6")
-        clip_weigh_x(1, 0)
+        clip_weigh_x(0, 1)
+        add_s(1, 0)
+        add_s(1, 1)
+        quantize(0, 0, 2)
         gather("scalar", 3, 0, 0, PASS)
         gather("scalar", 3, 1, 0, HALF)
-        gather("scalar", 3, 1, HALF, HALF)
-
-        weigh_x(1, 1)
-        weigh_g(1, 0)
+        gather("vector", 3, 1, HALF, HALF)
+        clip_weigh_x(1, 0)
+        weigh_g1(1, 0)
         turn_g(1, 0, "u2")
-        weigh_g_half(1, 1, 0)
-        weigh_g_half(1, 1, 1)
+        weigh_g1(1, 1)
         turn_g(1, 1, "u1")
-        quantize(2, 0, 2)
-        quantize(1, 0, 2)
-        quantize(0, 0, 2)
-        collect_g("scalar", 1, 0)
-        quantize(3, 0, 1)
-        collect_g("scalar", 1, 1)
-        multiply(0, 0, (1,))
-        multiply(0, 1, (1,))
+        clip_weigh_x(1, 1)
         multiply(0, 0, (0,))
         multiply(0, 1, (0,))
-        multiply(1, 0)
+        quantize(1, 0, 1)
+        collect_g("scalar", 1, 0)
+        quantize(3, 0, 1)
+        quantize(1, 1, 2)
+        collect_g("scalar", 1, 1)
+        multiply(1, 0, (0,))
+        multiply(0, 0, (1,))
+        multiply(1, 0, (1,))
+        multiply(0, 1, (1,))
         factor()
         quantize(3, 1, 2)
         multiply(1, 1)

@@ -16,8 +16,13 @@ ALU = mybir.AluOpType
 ACT = mybir.ActivationFunctionType
 
 P = 128
-PASS = 512
-HALF = 256
+PACK = 4
+PASS = P * PACK
+HALF = PASS // 2
+QUAD = 32
+LIST_COLUMN = 16
+LO_ROW = QUAD
+X0, X1, G0, G1 = 0, 1, 2, 3
 
 
 def tile_list_moment_over_listed_sums_kernel(tc, xf, ra, lo, gt, rb, gk, offs, offs2, out):
@@ -29,207 +34,202 @@ def tile_list_moment_over_listed_sums_kernel(tc, xf, ra, lo, gt, rb, gk, offs, o
         raw_rows = keep.tile([P, PASS], F32, name="raw_rows")
         nc.sync.dma_start(raw_rows[0:2, :], ra.rearrange("o (a j) -> (o a) j", a=2))
         nc.sync.dma_start(raw_rows[2:4, :], rb.rearrange("o (a j) -> (o a) j", a=2))
-        nc.sync.dma_start(raw_rows[32:33, 0:K], lo.rearrange("k o -> o k"))
+        nc.sync.dma_start(raw_rows[LO_ROW : LO_ROW + 1, 0:K], lo.rearrange("k o -> o k"))
 
         x_rows = xf.rearrange("(p c) t -> p c t", c=2)
         g_rows = gt.rearrange("(p h) v -> p h v", h=2)
-        table = [keep.tile([P, T], F32, name="table%d" % i, align_bytes=64) for i in range(4)]
-        x_list = keep.tile([P, J // 16], U16, name="x_list")
-        g_list = keep.tile([P, J // 16], U16, name="g_list")
+        table = [keep.tile([P, T], F32, name="table%d" % i, align_bytes=64) for i in (X0, X1, G0, G1)]
+        x_list = keep.tile([P, J // LIST_COLUMN], U16, name="x_list")
+        g_list = keep.tile([P, J // LIST_COLUMN], U16, name="g_list")
         gk_sb = keep.tile([P, 2], F32, name="gk_sb")
-        nc.sync.dma_start(table[2][:], g_rows[:, 0, :])
+        nc.sync.dma_start(table[G0][:], g_rows[:, 0, :])
         nc.sync.dma_start(g_list[:], offs2)
         nc.sync.dma_start(x_list[:], offs)
-        nc.sync.dma_start(table[0][:], x_rows[:, 0, :])
-        nc.sync.dma_start(table[1][:], x_rows[:, 1, :])
-        nc.sync.dma_start(table[3][:], g_rows[:, 1, :])
+        nc.sync.dma_start(table[X0][:], x_rows[:, 0, :])
+        nc.sync.dma_start(table[X1][:], x_rows[:, 1, :])
+        nc.sync.dma_start(table[G1][:], g_rows[:, 1, :])
         nc.sync.dma_start(gk_sb[:], gk.rearrange("(p c) o -> p (c o)", c=2))
         lists = [x_list, x_list, g_list, g_list]
 
-
-        staged = keep.tile([P, 4, P], F32, name="staged")
+        staged = keep.tile([P, PACK, P], F32, name="staged")
         zero = keep.tile([P, 1], F32, name="zero")
         nc.vector.memset(zero[:], 0.0)
-        ident = keep.tile([P, P], F32, name="ident")
-        nc.scalar.activation(ident[:], zero[:].to_broadcast([P, P]), ACT.Copy)
-        ones = keep.tile([P, 32], F32, name="ones")
+        nc.scalar.activation(staged[:, 0:2, :].rearrange("p t q -> p (t q)"), zero[:].to_broadcast([P, 2 * P]), ACT.Copy)
+
+        ones = keep.tile([P, QUAD], F32, name="ones")
         nc.vector.memset(ones[:], 1.0)
-        column = keep.tile([P, 32], F32, name="column", align_bytes=64)
+        column = keep.tile([P, QUAD], F32, name="column", align_bytes=64)
         nc.vector.tensor_tensor_scan(column[:], ones[:], ones[:], 0.0, ALU.mult, ALU.add)
-        row = keep.tile([P, 32], F32, name="row", align_bytes=64)
+        ident = keep.tile([P, P], F32, name="ident")
+        nc.vector.memset(ident[:], 0.0)
+        row = keep.tile([P, QUAD], F32, name="row", align_bytes=64)
         nc.vector.transpose(row[:], column[:])
-        nc.vector.memset(staged[:], 0.0)
-        for first in range(0, P, 32):
-            quad = slice(first, first + 32)
+        nc.vector.memset(staged[:, 2:4, :], 0.0)
+        for first in range(0, P, QUAD):
+            quad = slice(first, first + QUAD)
             nc.vector.tensor_tensor(ident[quad, quad], column[quad, :], row[quad, :], ALU.is_equal)
+
         nc.vector.tensor_copy(
             staged[0:4].rearrange("r t q -> r q t"),
-            raw_rows[0:4, :].rearrange("r (q t) -> r q t", t=4),
+            raw_rows[0:4, :].rearrange("r (q t) -> r q t", t=PACK),
         )
-        nc.vector.tensor_copy(staged[32:33, 0:2, :], raw_rows[32:33, 0:K].rearrange("r (p c) -> r c p", c=2))
-        turned = psum.tile([P, 4, P], F32, name="bank", tag="u1")
-        for t in range(4):
+        nc.scalar.activation(
+            staged[LO_ROW : LO_ROW + 1, 0:2, :],
+            raw_rows[LO_ROW : LO_ROW + 1, 0:K].rearrange("r (p c) -> r c p", c=2),
+            ACT.Copy,
+        )
+        turned = psum.tile([P, PACK, P], F32, name="turned", tag="bank_a")
+        for t in range(PACK):
             nc.tensor.transpose(turned[:, t, :], staged[:, t, :], ident[:])
-        weights = keep.tile([P, 4, 4], F32, name="weights")
-        nc.vector.tensor_copy(weights[:], turned[:, :, 0:4].rearrange("p t r -> p r t"))
+        weights = keep.tile([P, 4, PACK], F32, name="weights")
+        nc.scalar.activation(weights[:], turned[:, :, 0:4].rearrange("p t r -> p r t"), ACT.Copy)
         neg_lo = keep.tile([P, 2], F32, name="neg_lo")
-        nc.scalar.activation(neg_lo[:], turned[:, 0:2, 32], ACT.Copy, scale=-1.0)
-        row_factor = keep.tile([P, 2], F32, name="row_factor")
+        nc.scalar.activation(neg_lo[:], turned[:, 0:2, LO_ROW], ACT.Copy, scale=-1.0)
 
-        def factor():
-            nc.scalar.activation(row_factor[:], gk_sb[:], ACT.Copy, scale=0.02)
-
-        rb_wide = {}
-
-        def spread_rb(a, tag):
-            rb_wide[a] = psum.tile([P, 4, P], F32, name="bank", tag=tag)
-            for t in range(4):
+        rb_wide = [psum.tile([P, PACK, P], F32, name="rb_wide%d" % a) for a in range(2)]
+        for a in range(2):
+            for t in range(PACK):
                 nc.tensor.transpose(rb_wide[a][:, t, :], weights[:, 2 + a, t : t + 1].to_broadcast([P, P]), ident[:])
 
         picked = {(i, a): keep.tile([P, PASS], F32, name="picked%d%d" % (i, a), align_bytes=64)
-                  for i in range(4) for a in range(2)}
-        pairs = {(h, a): keep.tile([P, PASS], BF16, name="pairs%d%d" % (h, a)) for h in range(2) for a in range(2)}
-        whole = {i: keep.tile([P, J], BF16, name="grouped%d" % i, tag=tag, align_bytes=64)
-                 for i, tag in ((0, "grouped0"), (2, "table0"), (3, "grouped3"))}
-        grouped = {(i, a): whole[i][:, a * PASS : (a + 1) * PASS] for i in whole for a in range(2)}
+                  for i in (X0, X1, G0, G1) for a in range(2)}
+        pairs = {(i, a): keep.tile([P, PASS], BF16, name="pairs%d%d" % (i, a)) for i in (G0, G1) for a in range(2)}
+        both = {i: keep.tile([P, J], BF16, name="grouped%d" % i, tag=tag, align_bytes=64)
+                for i, tag in ((X0, "grouped0"), (G0, "table0"), (G1, "grouped3"))}
+        grouped = {(i, a): both[i][:, a * PASS : (a + 1) * PASS] for i in both for a in range(2)}
         for a, tag in ((0, "grouped1"), (1, "table3")):
-            grouped[(1, a)] = keep.tile([P, PASS], BF16, name="grouped1%d" % a, tag=tag, align_bytes=64)[:]
+            grouped[(X1, a)] = keep.tile([P, PASS], BF16, name="grouped1%d" % a, tag=tag, align_bytes=64)[:]
         code_tags = ["codes0", "picked31", "codes2", "codes3"]
-        codes = [keep.tile([P, 2 * P], U32, name="codes%d" % i, tag=code_tags[i], align_bytes=64) for i in range(4)]
-        scales = [keep.tile([P, 2 * P], U8, name="scales%d" % i, align_bytes=64) for i in range(4)]
-        acc = {}
+        codes = [keep.tile([P, 2 * P], U32, name="codes%d" % i, tag=code_tags[i], align_bytes=64)
+                 for i in (X0, X1, G0, G1)]
+        scales = [keep.tile([P, 2 * P], U8, name="scales%d" % i, align_bytes=64) for i in (X0, X1, G0, G1)]
         banks = {}
+        moment = {}
 
         def gather(engine, i, a, start, count):
             first = a * PASS + start
-            window = table[i][:].indirect(lists[i][:, first // 16 : (first + count) // 16])
+            window = table[i][:].indirect(lists[i][:, first // LIST_COLUMN : (first + count) // LIST_COLUMN])
             dst = picked[(i, a)][:, start : start + count]
             if engine == "vector":
                 nc.vector.tensor_copy(dst, window)
             else:
                 nc.scalar.activation(dst, window, ACT.Copy)
 
-        def weigh_g1(h, a):
-            nc.vector.tensor_tensor(
-                pairs[(h, a)][:].rearrange("p (q t) -> p q t", t=4),
-                picked[(2 + h, a)][:].rearrange("p (q t) -> p q t", t=4),
-                rb_wide[a][:].rearrange("p t q -> p q t"),
-                ALU.mult,
-            )
+        def gather_shared(i):
+            for a in range(2):
+                gather("vector", i, a, 0, HALF)
+                gather("scalar", i, a, HALF, HALF)
 
-        def turn_g(h, a, tag):
-            bank = psum.tile([P, 4, P], F32, name="bank", tag=tag)
-            words = pairs[(h, a)][:].bitcast(F32)
-            for u in range(2):
-                nc.tensor.transpose(bank[:, u, :], words[:, u:HALF:2], ident[:])
-            banks[(2 + h, a)] = bank
-
-        def collect_g(engine, h, a):
-            dst = grouped[(2 + h, a)].bitcast(F32).rearrange("p (n u) -> p n u", u=2)
-            src = banks[(2 + h, a)][:, 0:2, :].rearrange("p u n -> p n u")
-            if engine == "vector":
-                nc.vector.tensor_copy(dst, src)
-            else:
-                nc.scalar.copy(dst, src)
-
-        def quantize(i, first, last):
-            fmt = E4M3 if i < 2 else E5M2
-            nc.vector.quantize_mx(
-                out=codes[i][:, first * P : last * P].bitcast(fmt),
-                scales=scales[i][:, first * P : last * P],
-                in_=whole[i][:] if last - first == 2 else grouped[(i, first)],
-            )
-
-        def multiply(h, a, cs=(0, 1)):
-            for c in cs:
-                if c not in acc:
-                    acc[c] = psum.tile([P, P], F32, name="acc%d" % c, tag="acc%d" % c)
-                nc.tensor.matmul_mx(
-                    out=acc[c][:],
-                    lhsT=codes[c][:, a * P : (a + 1) * P].bitcast(E4M3),
-                    lhsT_scale=scales[c][:, a * P : (a + 1) * P],
-                    rhs=codes[2 + h][:, a * P : (a + 1) * P].bitcast(E5M2),
-                    rhs_scale=scales[2 + h][:, a * P : (a + 1) * P],
-                    start=(h == 0 and a == 0),
-                    stop=(h == 1 and a == 1),
-                )
-
-        def open_x(c, a, tag):
-            bank = psum.tile([P, 4, P], F32, name="bank", tag=tag)
-            for t in range(4):
-                nc.tensor.matmul(bank[:, t, :], neg_lo[:, c : c + 1].to_broadcast([P, P]), ident[:],
+        def open_x(i, a, tag):
+            bank = psum.tile([P, PACK, P], F32, name="x_bank", tag=tag)
+            for t in range(PACK):
+                nc.tensor.matmul(bank[:, t, :], neg_lo[:, i : i + 1].to_broadcast([P, P]), ident[:],
                                  is_transpose=True, start=(t == 0), stop=False)
-            banks[(c, a)] = bank
+            banks[(i, a)] = bank
 
-        def add_s(c, a):
-            for t in range(4):
-                nc.tensor.matmul(banks[(c, a)][:, t, :], picked[(c, a)][:, t:PASS:4], ident[:],
-                                 is_transpose=True, start=False, stop=(t == 3))
+        def turn_x(i, a):
+            for t in range(PACK):
+                nc.tensor.matmul(banks[(i, a)][:, t, :], picked[(i, a)][:, t:PASS:PACK], ident[:],
+                                 is_transpose=True, start=False, stop=(t == PACK - 1))
 
-        def clip_weigh_x(c, a):
+        def weigh_x(i, a):
             nc.vector.scalar_tensor_tensor(
-                grouped[(c, a)].rearrange("p (k t) -> p k t", t=4),
-                banks[(c, a)][:].rearrange("p t k -> p k t"),
+                grouped[(i, a)].rearrange("p (k t) -> p k t", t=PACK),
+                banks[(i, a)][:].rearrange("p t k -> p k t"),
                 0.0,
-                weights[:, a : a + 1, :].to_broadcast([P, P, 4]),
+                weights[:, a : a + 1, :].to_broadcast([P, P, PACK]),
                 ALU.max,
                 ALU.mult,
             )
 
-        spread_rb(0, "u3")
-        spread_rb(1, "u4")
-        gather("vector", 2, 0, 0, PASS)
-        gather("scalar", 2, 1, 0, PASS)
-        weigh_g1(0, 0)
-        turn_g(0, 0, "u1")
-        weigh_g1(0, 1)
-        turn_g(0, 1, "u6")
-        open_x(0, 0, "u2")
-        open_x(0, 1, "acc0")
-        open_x(1, 0, "u5")
-        open_x(1, 1, "acc1")
-        gather("vector", 0, 0, 0, PASS)
-        gather("scalar", 0, 1, 0, PASS)
-        add_s(0, 0)
-        add_s(0, 1)
-        collect_g("vector", 0, 0)
-        collect_g("vector", 0, 1)
-        quantize(2, 0, 2)
-        gather("scalar", 1, 0, 0, PASS)
-        gather("scalar", 1, 1, 0, PASS)
-        clip_weigh_x(0, 0)
-        clip_weigh_x(0, 1)
-        add_s(1, 0)
-        add_s(1, 1)
-        quantize(0, 0, 2)
-        gather("scalar", 3, 0, 0, PASS)
-        gather("scalar", 3, 1, 0, HALF)
-        gather("vector", 3, 1, HALF, HALF)
-        clip_weigh_x(1, 0)
-        weigh_g1(1, 0)
-        turn_g(1, 0, "u2")
-        weigh_g1(1, 1)
-        turn_g(1, 1, "u1")
-        clip_weigh_x(1, 1)
-        multiply(0, 0, (0,))
-        multiply(0, 1, (0,))
-        quantize(1, 0, 1)
-        collect_g("scalar", 1, 0)
-        quantize(3, 0, 1)
-        quantize(1, 1, 2)
-        collect_g("scalar", 1, 1)
-        multiply(1, 0, (0,))
-        multiply(0, 0, (1,))
-        multiply(1, 0, (1,))
-        multiply(0, 1, (1,))
-        factor()
-        quantize(3, 1, 2)
-        multiply(1, 1)
+        def weigh_and_turn_g(i, a, tag):
+            nc.vector.tensor_tensor(
+                pairs[(i, a)][:].rearrange("p (q t) -> p q t", t=PACK),
+                picked[(i, a)][:].rearrange("p (q t) -> p q t", t=PACK),
+                rb_wide[a][:].rearrange("p t q -> p q t"),
+                ALU.mult,
+            )
+            bank = psum.tile([P, PACK, P], F32, name="g_bank", tag=tag)
+            words = pairs[(i, a)][:].bitcast(F32)
+            for u in range(2):
+                nc.tensor.transpose(bank[:, u, :], words[:, u:HALF:2], ident[:])
+            banks[(i, a)] = bank
+
+        def collect_g(copy, i, a):
+            copy(grouped[(i, a)].bitcast(F32).rearrange("p (n u) -> p n u", u=2),
+                 banks[(i, a)][:, 0:2, :].rearrange("p u n -> p n u"))
+
+        def quantize(i, source, first, last):
+            nc.vector.quantize_mx(
+                out=codes[i][:, first * P : last * P].bitcast(E4M3 if i in (X0, X1) else E5M2),
+                scales=scales[i][:, first * P : last * P],
+                in_=source,
+            )
+
+        def multiply(xi, gi, a):
+            cols = slice(a * P, (a + 1) * P)
+            nc.tensor.matmul_mx(
+                out=moment[xi][:],
+                lhsT=codes[xi][:, cols].bitcast(E4M3),
+                lhsT_scale=scales[xi][:, cols],
+                rhs=codes[gi][:, cols].bitcast(E5M2),
+                rhs_scale=scales[gi][:, cols],
+                start=(gi == G0 and a == 0),
+                stop=(gi == G1 and a == 1),
+            )
+
+        gather_shared(G0)
+        weigh_and_turn_g(G0, 0, "bank_a")
+        weigh_and_turn_g(G0, 1, "bank_b")
+        for i, a, tag in ((X0, 0, "bank_c"), (X0, 1, "bank_d"), (X1, 0, "bank_e"), (X1, 1, "bank_f")):
+            open_x(i, a, tag)
+
+        gather_shared(X0)
+        for a in range(2):
+            turn_x(X0, a)
+        for a in range(2):
+            collect_g(nc.vector.tensor_copy, G0, a)
+        quantize(G0, both[G0][:], 0, 2)
+
+        for a in range(2):
+            gather("scalar", X1, a, 0, PASS)
+        for a in range(2):
+            weigh_x(X0, a)
+        for a in range(2):
+            turn_x(X1, a)
+        quantize(X0, both[X0][:], 0, 2)
+
+        gather("scalar", G1, 0, 0, PASS)
+        gather("scalar", G1, 1, 0, HALF)
+        gather("vector", G1, 1, HALF, HALF)
+        weigh_x(X1, 0)
+        weigh_and_turn_g(G1, 0, "bank_c")
+        weigh_and_turn_g(G1, 1, "bank_a")
+        weigh_x(X1, 1)
+
+        moment[X0] = psum.tile([P, P], F32, name="moment0", tag="bank_d")
+        multiply(X0, G0, 0)
+        multiply(X0, G0, 1)
+        quantize(X1, grouped[(X1, 0)], 0, 1)
+        collect_g(nc.scalar.copy, G1, 0)
+        quantize(G1, grouped[(G1, 0)], 0, 1)
+        quantize(X1, grouped[(X1, 1)], 1, 2)
+        collect_g(nc.scalar.copy, G1, 1)
+        multiply(X0, G1, 0)
+        moment[X1] = psum.tile([P, P], F32, name="moment1", tag="bank_f")
+        multiply(X1, G0, 0)
+        multiply(X1, G1, 0)
+        multiply(X1, G0, 1)
+        row_factor = keep.tile([P, 2], F32, name="row_factor")
+        nc.scalar.activation(row_factor[:], gk_sb[:], ACT.Copy, scale=0.02)
+        quantize(G1, grouped[(G1, 1)], 1, 2)
+        multiply(X0, G1, 1)
+        multiply(X1, G1, 1)
 
         scaled = keep.tile([P, 2, P], F32, name="scaled")
-        nc.scalar.activation(scaled[:, 0, :], acc[0][:], ACT.Copy, scale=row_factor[:, 0:1])
-        nc.vector.tensor_scalar(scaled[:, 1, :], acc[1][:], row_factor[:, 1:2], None, ALU.mult)
+        nc.scalar.activation(scaled[:, X0, :], moment[X0][:], ACT.Copy, scale=row_factor[:, X0 : X0 + 1])
+        nc.vector.tensor_scalar(scaled[:, X1, :], moment[X1][:], row_factor[:, X1 : X1 + 1], None, ALU.mult)
         result = keep.tile([P, 2 * Q], F32, name="result")
-        halves = scaled[:].rearrange("p c (q e) -> p (c q) e", e=2)
-        nc.vector.tensor_tensor(result[:], halves[:, :, 0], halves[:, :, 1], ALU.add)
+        neighbours = scaled[:].rearrange("p c (q e) -> p (c q) e", e=2)
+        nc.vector.tensor_tensor(result[:], neighbours[:, :, 0], neighbours[:, :, 1], ALU.add)
         nc.sync.dma_start(out.rearrange("(p c) q -> p (c q)", c=2), result[:])

from contextlib import ExitStack

import concourse.mybir as mybir

K, J, N, T, Q = 256, 1024, 256, 2048, 64
FLOPS = 2 * K * J * N

F32 = mybir.dt.float32
BF16 = mybir.dt.bfloat16
U32 = mybir.dt.uint32
U16 = mybir.dt.uint16
U8 = mybir.dt.uint8
E4M3 = mybir.dt.float8_e4m3fn_x4
E5M2 = mybir.dt.float8_e5m2_x4
ALU = mybir.AluOpType
ACT = mybir.ActivationFunctionType

P = 128
PACK = 4
PASS = P * PACK
HALF = PASS // 2
QUAD = 32
LIST_COLUMN = 16
LO_ROW = QUAD
X0, X1, G0, G1 = 0, 1, 2, 3


def tile_list_moment_over_listed_sums_kernel(tc, xf, ra, lo, gt, rb, gk, offs, offs2, out):
    nc = tc.nc
    with ExitStack() as ctx:
        keep = ctx.enter_context(tc.tile_pool(name="keep", bufs=1))
        psum = ctx.enter_context(tc.psum_pool(name="psum", bufs=1))

        raw_rows = keep.tile([P, PASS], F32, name="raw_rows")
        nc.sync.dma_start(raw_rows[0:2, :], ra.rearrange("o (a j) -> (o a) j", a=2))
        nc.sync.dma_start(raw_rows[2:4, :], rb.rearrange("o (a j) -> (o a) j", a=2))
        nc.sync.dma_start(raw_rows[LO_ROW : LO_ROW + 1, 0:K], lo.rearrange("k o -> o k"))

        x_rows = xf.rearrange("(p c) t -> p c t", c=2)
        g_rows = gt.rearrange("(p h) v -> p h v", h=2)
        table = [keep.tile([P, T], F32, name="table%d" % i, align_bytes=64) for i in (X0, X1, G0, G1)]
        x_list = keep.tile([P, J // LIST_COLUMN], U16, name="x_list")
        g_list = keep.tile([P, J // LIST_COLUMN], U16, name="g_list")
        gk_sb = keep.tile([P, 2], F32, name="gk_sb")
        nc.sync.dma_start(table[G0][:], g_rows[:, 0, :])
        nc.sync.dma_start(g_list[:], offs2)
        nc.sync.dma_start(x_list[:], offs)
        nc.sync.dma_start(table[X0][:], x_rows[:, 0, :])
        nc.sync.dma_start(table[X1][:], x_rows[:, 1, :])
        nc.sync.dma_start(table[G1][:], g_rows[:, 1, :])
        nc.sync.dma_start(gk_sb[:], gk.rearrange("(p c) o -> p (c o)", c=2))
        lists = [x_list, x_list, g_list, g_list]

        staged = keep.tile([P, PACK, P], F32, name="staged")
        zero = keep.tile([P, 1], F32, name="zero")
        nc.vector.memset(zero[:], 0.0)
        nc.scalar.activation(staged[:, 0:2, :].rearrange("p t q -> p (t q)"), zero[:].to_broadcast([P, 2 * P]), ACT.Copy)

        ones = keep.tile([P, QUAD], F32, name="ones")
        nc.vector.memset(ones[:], 1.0)
        column = keep.tile([P, QUAD], F32, name="column", align_bytes=64)
        nc.vector.tensor_tensor_scan(column[:], ones[:], ones[:], 0.0, ALU.mult, ALU.add)
        ident = keep.tile([P, P], F32, name="ident")
        nc.vector.memset(ident[:], 0.0)
        row = keep.tile([P, QUAD], F32, name="row", align_bytes=64)
        nc.vector.transpose(row[:], column[:])
        nc.vector.memset(staged[:, 2:4, :], 0.0)
        for first in range(0, P, QUAD):
            quad = slice(first, first + QUAD)
            nc.vector.tensor_tensor(ident[quad, quad], column[quad, :], row[quad, :], ALU.is_equal)

        nc.vector.tensor_copy(
            staged[0:4].rearrange("r t q -> r q t"),
            raw_rows[0:4, :].rearrange("r (q t) -> r q t", t=PACK),
        )
        nc.scalar.activation(
            staged[LO_ROW : LO_ROW + 1, 0:2, :],
            raw_rows[LO_ROW : LO_ROW + 1, 0:K].rearrange("r (p c) -> r c p", c=2),
            ACT.Copy,
        )
        turned = psum.tile([P, PACK, P], F32, name="turned", tag="bank_a")
        for t in range(PACK):
            nc.tensor.transpose(turned[:, t, :], staged[:, t, :], ident[:])
        weights = keep.tile([P, 4, PACK], F32, name="weights")
        nc.scalar.activation(weights[:], turned[:, :, 0:4].rearrange("p t r -> p r t"), ACT.Copy)
        neg_lo = keep.tile([P, 2], F32, name="neg_lo")
        nc.scalar.activation(neg_lo[:], turned[:, 0:2, LO_ROW], ACT.Copy, scale=-1.0)

        rb_wide = [psum.tile([P, PACK, P], F32, name="rb_wide%d" % a) for a in range(2)]
        for a in range(2):
            for t in range(PACK):
                nc.tensor.transpose(rb_wide[a][:, t, :], weights[:, 2 + a, t : t + 1].to_broadcast([P, P]), ident[:])

        picked = {(i, a): keep.tile([P, PASS], F32, name="picked%d%d" % (i, a), align_bytes=64)
                  for i in (X0, X1, G0, G1) for a in range(2)}
        pairs = {(i, a): keep.tile([P, PASS], BF16, name="pairs%d%d" % (i, a)) for i in (G0, G1) for a in range(2)}
        both = {i: keep.tile([P, J], BF16, name="grouped%d" % i, tag=tag, align_bytes=64)
                for i, tag in ((X0, "grouped0"), (G0, "table0"), (G1, "grouped3"))}
        grouped = {(i, a): both[i][:, a * PASS : (a + 1) * PASS] for i in both for a in range(2)}
        for a, tag in ((0, "grouped1"), (1, "table3")):
            grouped[(X1, a)] = keep.tile([P, PASS], BF16, name="grouped1%d" % a, tag=tag, align_bytes=64)[:]
        code_tags = ["codes0", "picked31", "codes2", "codes3"]
        codes = [keep.tile([P, 2 * P], U32, name="codes%d" % i, tag=code_tags[i], align_bytes=64)
                 for i in (X0, X1, G0, G1)]
        scales = [keep.tile([P, 2 * P], U8, name="scales%d" % i, align_bytes=64) for i in (X0, X1, G0, G1)]
        banks = {}
        moment = {}

        def gather(engine, i, a, start, count):
            first = a * PASS + start
            window = table[i][:].indirect(lists[i][:, first // LIST_COLUMN : (first + count) // LIST_COLUMN])
            dst = picked[(i, a)][:, start : start + count]
            if engine == "vector":
                nc.vector.tensor_copy(dst, window)
            else:
                nc.scalar.activation(dst, window, ACT.Copy)

        def gather_shared(i):
            for a in range(2):
                gather("vector", i, a, 0, HALF)
                gather("scalar", i, a, HALF, HALF)

        def open_x(i, a, tag):
            bank = psum.tile([P, PACK, P], F32, name="x_bank", tag=tag)
            for t in range(PACK):
                nc.tensor.matmul(bank[:, t, :], neg_lo[:, i : i + 1].to_broadcast([P, P]), ident[:],
                                 is_transpose=True, start=(t == 0), stop=False)
            banks[(i, a)] = bank

        def turn_x(i, a):
            for t in range(PACK):
                nc.tensor.matmul(banks[(i, a)][:, t, :], picked[(i, a)][:, t:PASS:PACK], ident[:],
                                 is_transpose=True, start=False, stop=(t == PACK - 1))

        def weigh_x(i, a):
            nc.vector.scalar_tensor_tensor(
                grouped[(i, a)].rearrange("p (k t) -> p k t", t=PACK),
                banks[(i, a)][:].rearrange("p t k -> p k t"),
                0.0,
                weights[:, a : a + 1, :].to_broadcast([P, P, PACK]),
                ALU.max,
                ALU.mult,
            )

        def weigh_and_turn_g(i, a, tag):
            nc.vector.tensor_tensor(
                pairs[(i, a)][:].rearrange("p (q t) -> p q t", t=PACK),
                picked[(i, a)][:].rearrange("p (q t) -> p q t", t=PACK),
                rb_wide[a][:].rearrange("p t q -> p q t"),
                ALU.mult,
            )
            bank = psum.tile([P, PACK, P], F32, name="g_bank", tag=tag)
            words = pairs[(i, a)][:].bitcast(F32)
            for u in range(2):
                nc.tensor.transpose(bank[:, u, :], words[:, u:HALF:2], ident[:])
            banks[(i, a)] = bank

        def collect_g(copy, i, a):
            copy(grouped[(i, a)].bitcast(F32).rearrange("p (n u) -> p n u", u=2),
                 banks[(i, a)][:, 0:2, :].rearrange("p u n -> p n u"))

        def quantize(i, source, first, last):
            nc.vector.quantize_mx(
                out=codes[i][:, first * P : last * P].bitcast(E4M3 if i in (X0, X1) else E5M2),
                scales=scales[i][:, first * P : last * P],
                in_=source,
            )

        def multiply(xi, gi, a):
            cols = slice(a * P, (a + 1) * P)
            nc.tensor.matmul_mx(
                out=moment[xi][:],
                lhsT=codes[xi][:, cols].bitcast(E4M3),
                lhsT_scale=scales[xi][:, cols],
                rhs=codes[gi][:, cols].bitcast(E5M2),
                rhs_scale=scales[gi][:, cols],
                start=(gi == G0 and a == 0),
                stop=(gi == G1 and a == 1),
            )

        gather_shared(G0)
        weigh_and_turn_g(G0, 0, "bank_a")
        weigh_and_turn_g(G0, 1, "bank_b")
        for i, a, tag in ((X0, 0, "bank_c"), (X0, 1, "bank_d"), (X1, 0, "bank_e"), (X1, 1, "bank_f")):
            open_x(i, a, tag)

        gather_shared(X0)
        for a in range(2):
            turn_x(X0, a)
        for a in range(2):
            collect_g(nc.vector.tensor_copy, G0, a)
        quantize(G0, both[G0][:], 0, 2)

        for a in range(2):
            gather("scalar", X1, a, 0, PASS)
        for a in range(2):
            weigh_x(X0, a)
        for a in range(2):
            turn_x(X1, a)
        quantize(X0, both[X0][:], 0, 2)

        gather("scalar", G1, 0, 0, PASS)
        gather("scalar", G1, 1, 0, HALF)
        gather("vector", G1, 1, HALF, HALF)
        weigh_x(X1, 0)
        weigh_and_turn_g(G1, 0, "bank_c")
        weigh_and_turn_g(G1, 1, "bank_a")
        weigh_x(X1, 1)

        moment[X0] = psum.tile([P, P], F32, name="moment0", tag="bank_d")
        multiply(X0, G0, 0)
        multiply(X0, G0, 1)
        quantize(X1, grouped[(X1, 0)], 0, 1)
        collect_g(nc.scalar.copy, G1, 0)
        quantize(G1, grouped[(G1, 0)], 0, 1)
        quantize(X1, grouped[(X1, 1)], 1, 2)
        collect_g(nc.scalar.copy, G1, 1)
        multiply(X0, G1, 0)
        moment[X1] = psum.tile([P, P], F32, name="moment1", tag="bank_f")
        multiply(X1, G0, 0)
        multiply(X1, G1, 0)
        multiply(X1, G0, 1)
        row_factor = keep.tile([P, 2], F32, name="row_factor")
        nc.scalar.activation(row_factor[:], gk_sb[:], ACT.Copy, scale=0.02)
        quantize(G1, grouped[(G1, 1)], 1, 2)
        multiply(X0, G1, 1)
        multiply(X1, G1, 1)

        scaled = keep.tile([P, 2, P], F32, name="scaled")
        nc.scalar.activation(scaled[:, X0, :], moment[X0][:], ACT.Copy, scale=row_factor[:, X0 : X0 + 1])
        nc.vector.tensor_scalar(scaled[:, X1, :], moment[X1][:], row_factor[:, X1 : X1 + 1], None, ALU.mult)
        result = keep.tile([P, 2 * Q], F32, name="result")
        neighbours = scaled[:].rearrange("p c (q e) -> p (c q) e", e=2)
        nc.vector.tensor_tensor(result[:], neighbours[:, :, 0], neighbours[:, :, 1], ALU.add)
        nc.sync.dma_start(out.rearrange("(p c) q -> p (c q)", c=2), result[:])
